import numpy as np
import ml_dtypes


def mxq(x, axis, fmt="e4m3"):
    dtype, down = {"e4m3": (ml_dtypes.float8_e4m3fn, 7), "e5m2": (ml_dtypes.float8_e5m2, 14)}[fmt]
    v = np.moveaxis(np.asarray(x, np.float32).astype(ml_dtypes.bfloat16).astype(np.float64), axis, -1)
    blocks = v.reshape(v.shape[:-1] + (-1, 32))
    amax = np.abs(blocks).max(-1, keepdims=True)
    byte = np.maximum(np.where(amax > 0, np.frexp(amax)[1] - 1 + 127, 0) - down, 1)
    scale = np.exp2(byte - 127.0)
    codes = (blocks / scale).astype(np.float32).astype(dtype).astype(np.float64)
    return np.moveaxis((codes * scale).reshape(v.shape), -1, axis)


WIDE = False


def mx_kscale(k):
    if not WIDE:
        return np.ones(k)
    levels = np.array([10, -10, 5, -5, 0])
    if k % 512:
        return np.exp2(np.random.permutation(np.resize(levels, k // 32))).repeat(32)
    a = np.empty((k // 512, 16))
    for p in range(k // 512):
        a[p, :8] = np.random.permutation(np.resize(levels, 8))
        for g in range(8):
            far = levels[np.abs(levels - a[p, g]) >= 10]
            a[p, g + 8] = far[np.random.randint(len(far))]
    return np.exp2(a.ravel()).repeat(32)


def f64(x):
    return np.asarray(x).astype(np.float64)


def striped(idx):
    return np.tile(idx.reshape(-1, 16).T, (8, 1)).astype(np.uint16)


def unstriped(offs):
    return offs[:16].T.reshape(-1).astype(np.int64)


E2M1 = np.array([0.0, 0.5, 1.0, 1.5, 2.0, 3.0, 4.0, 6.0, -0.0, -0.5, -1.0, -1.5, -2.0, -3.0, -4.0, -6.0])


def pack_weight(w, fmt):
    k, n = w.shape
    w = f64(np.asarray(w, np.float32).astype(ml_dtypes.bfloat16)).reshape(k // 32, 32, n)
    amax = np.abs(w).max(1)
    if fmt == "e4m3":
        byte = np.frexp(amax)[1] - 1 + 127 - 7
    else:
        mant, ex = np.frexp(amax / 6.0)
        byte = np.where(mant > 0.5, ex, ex - 1) + 127
    byte = np.clip(np.where(amax > 0, byte, 1), 1, 254)
    scaled = (w * np.exp2(127.0 - byte)[:, None, :]).reshape(k, n).astype(np.float32)
    by_word = np.ascontiguousarray(scaled.reshape(k // 512, 128, 4, n).transpose(0, 1, 3, 2))
    if fmt == "e4m3":
        words = by_word.astype(ml_dtypes.float8_e4m3fn).view(np.uint8)
    else:
        c = by_word.astype(ml_dtypes.float4_e2m1fn).view(np.uint8) & 0xF
        words = (c[..., 0::2] | (c[..., 1::2] << 4)).reshape(k // 512, 128, 2 * n)
    return np.ascontiguousarray(words), np.ascontiguousarray(byte.astype(np.uint8).reshape(k // 512, 16, n))


def unpack_weight(words, scales, fmt):
    g, _, n = scales.shape
    words = np.ascontiguousarray(words).reshape(g, 128, n, -1)
    if fmt == "e4m3":
        vals = words.view(ml_dtypes.float8_e4m3fn).astype(np.float64)
    else:
        nib = np.empty((g, 128, n, 4), np.uint8)
        nib[..., 0::2] = words & 0xF
        nib[..., 1::2] = words >> 4
        vals = E2M1[nib]
    vals = vals * np.repeat(np.exp2(scales.astype(np.float64) - 127.0), 8, axis=1)[..., None]
    return vals.transpose(0, 1, 3, 2).reshape(g * 512, n)


def gelu(v):
    return 0.5 * v * (1.0 + np.tanh(np.sqrt(2.0 / np.pi) * (v + 0.044715 * v**3)))


K, H, N, T, S = 1024, 512, 512, 2048, 1024

def setup_inputs():
    n = np.random.standard_normal
    s = mx_kscale(K)[:, None]
    u = mx_kscale(H)[:, None]
    tab_words, tab_scales = pack_weight(n((K, T)) * s, "e4m3")
    w2_words, w2_scales = pack_weight(n((K, H)) / np.sqrt(K) / s * u.T, "e2m1")
    w3_words, w3_scales = pack_weight(n((K, H)) / np.sqrt(K) / s, "e4m3")
    return {
        "tab_words": tab_words, "tab_scales": tab_scales,
        "offs": striped(np.random.permutation(T)[:S]),
        "offs2": striped(np.random.permutation(T)[:S]),
        "offs3": striped(np.random.permutation(T)[:S]),
        "w1": (n((K, H)) / np.sqrt(K) / s * u.T).astype(np.float32),
        "w2_words": w2_words, "w2_scales": w2_scales,
        "w3_words": w3_words, "w3_scales": w3_scales,
        "m": (n((H, N)) / np.sqrt(H) / u).astype(np.float32),
        "src": (0.5 * n(N)).astype(np.float32),
    }

def reference(tab_words, tab_scales, offs, offs2, offs3, w1, w2_words, w2_scales, w3_words, w3_scales, m, src):
    vc = unpack_weight(tab_words, tab_scales, "e4m3")[:, unstriped(offs)]
    vn = unpack_weight(tab_words, tab_scales, "e4m3")[:, unstriped(offs2)]
    vd = unpack_weight(tab_words, tab_scales, "e4m3")[:, unstriped(offs3)]
    w2 = unpack_weight(w2_words, w2_scales, "e2m1")
    w3 = unpack_weight(w3_words, w3_scales, "e4m3")
    a = mxq(f64(w1), 0, "e4m3").T @ vc
    b = w2.T @ vn
    c = w3.T @ vd
    h = (a - b) / (1.0 + np.square(c))
    y = mxq(f64(m), 0, "e4m3").T @ mxq(h, 0, "e4m3")
    return y + f64(src)[:, None]

@@ -1,0 +1,302 @@
+from contextlib import ExitStack
+
+import concourse.mybir as mybir
+
+K, H, N, T, S = 1024, 512, 512, 2048, 1024
+FLOPS = 2 * (3 * K * H * S + H * N * S)
+
+F32 = mybir.dt.float32
+BF16 = mybir.dt.bfloat16
+I32 = mybir.dt.int32
+U32 = mybir.dt.uint32
+U16 = mybir.dt.uint16
+U8 = mybir.dt.uint8
+FP8X4 = mybir.dt.float8_e4m3fn_x4
+FP4X4 = mybir.dt.float4_e2m1fn_x4
+ACT = mybir.ActivationFunctionType
+ALU = mybir.AluOpType
+
+P = 128
+PACK = 4
+PASSES = K // (P * PACK)
+QUADS = 4
+CHUNK = 128
+GROUP = 256
+GROUPS = S // GROUP
+PER = GROUP // CHUNK
+WIDTH = PACK * CHUNK
+
+
+def tile_list_damped_mesh_flux_kernel(
+    tc, tab_words, tab_scales, offs, offs2, offs3, w1, w2_words, w2_scales, w3_words, w3_scales, m, src, out
+):
+    nc = tc.nc
+    with ExitStack() as ctx:
+        keep = ctx.enter_context(tc.tile_pool(name="keep", bufs=1))
+        ring = ctx.enter_context(tc.tile_pool(name="ring", bufs=2))
+        psum = ctx.enter_context(tc.psum_pool(name="psum", bufs=2))
+
+        def held(shape, dtype, name):
+            return keep.tile(shape, dtype, name=name, align_bytes=64)
+
+        lists = {name: held([P, S // 16], U16, "list_" + name) for name in "cba"}
+
+        tab_plane = held([P, T], U8, "tab_plane")
+        nc.vector.memset(tab_plane[:].bitcast(I32), 0)
+        w3_stage = held([P, PASSES * (H + H // 4)], I32, "words_c")
+        w2_stage = held([P, PASSES * (H // 2 + H // 4)], I32, "words_b")
+        w3_raw = w3_stage[:, : PASSES * H].rearrange("p (a e) -> p a e", a=PASSES)
+        w3_plane_raw = w3_stage[:, PASSES * H :].rearrange("p (a e) -> p a e", a=PASSES)
+        w2_raw = w2_stage[:, : PASSES * H // 2].rearrange("p (a e) -> p a e", a=PASSES)
+        w2_plane_raw = w2_stage[:, PASSES * H // 2 :].rearrange("p (a e) -> p a e", a=PASSES)
+        b_plane1 = held([P, S], U8, "b_plane1")
+        nc.vector.memset(w3_stage[:, PASSES * H :], 0)
+        nc.vector.memset(w2_stage[:, PASSES * H // 2 :], 0)
+        nc.gpsimd.memset(b_plane1[:].bitcast(I32), 0)
+
+        nc.sync.dma_start(lists["c"][:], offs3)
+        nc.sync.dma_start(lists["b"][:], offs2)
+        nc.sync.dma_start(lists["a"][:], offs)
+        for q in range(QUADS):
+            nc.sync.dma_start(
+                out=tab_plane[32 * q : 32 * q + 8, :].bitcast(I32),
+                in_=tab_scales[:, 4 * q : 4 * q + 4, :].bitcast(I32),
+            )
+        tab = held([P, PASSES, T], U32, "tab")
+        nc.sync.dma_start(out=tab[:].bitcast(I32), in_=tab_words.rearrange("a p t i -> p a (t i)").bitcast(I32))
+
+        def load_plane(raw, scales):
+            for q in range(QUADS):
+                nc.sync.dma_start(
+                    out=raw[32 * q : 32 * q + 4, :, :],
+                    in_=scales[:, 4 * q : 4 * q + 4, :].rearrange("a r e -> r a e").bitcast(I32),
+                )
+
+        nc.sync.dma_start(out=w3_raw, in_=w3_words.rearrange("a p e i -> p a (e i)").bitcast(I32))
+        load_plane(w3_plane_raw, w3_scales)
+        nc.sync.dma_start(out=w2_raw, in_=w2_words.rearrange("a p e -> p a e").bitcast(I32))
+        load_plane(w2_plane_raw, w2_scales)
+        w1_raw = []
+        for a in range(PASSES):
+            raw = held([P, PACK, H], F32, "w1_raw%d" % a)
+            nc.sync.dma_start(out=raw[:], in_=w1[512 * a : 512 * (a + 1), :].rearrange("(p j) c -> p j c", j=PACK))
+            w1_raw.append(raw)
+
+        planes = {}
+
+        def gather_plane(name, tag):
+            planes[name] = held([P, S], U8, tag)
+            nc.vector.tensor_copy(out=planes[name][:], in_=tab_plane[:].indirect(lists[name][:]))
+
+        gather_plane("c", "plane_c")
+        gather_plane("b", "plane_b")
+        for q in range(QUADS):
+            nc.sync.dma_start(
+                out=b_plane1[32 * q : 32 * q + 4, :].bitcast(I32),
+                in_=planes["b"][32 * q + 4 : 32 * q + 8, :].bitcast(I32),
+            )
+        m_raw = held([P, PACK, N], F32, "m_raw")
+        m_rows = m.rearrange("(q t e) n -> e q t n", t=4, e=4)
+        for e in range(4):
+            nc.sync.dma_start(out=m_raw[e:P:4, :, :], in_=m_rows[e])
+        src_col = held([P, N // P], F32, "src_col")
+        with nc.allow_non_contiguous_dma(reason="one source value for each partition and output tile"):
+            nc.sync.dma_start(out=src_col[:], in_=src.rearrange("(t p) -> p t", p=P))
+
+        def deal(dst, source, run):
+            nc.vector.tensor_copy(
+                out=dst.rearrange("p a (t q e) -> p a t q e", t=4, e=run),
+                in_=source.rearrange("p a (q t e) -> p a t q e", t=4, e=run),
+            )
+
+        w3_codes = held([P, PASSES, H], U32, "w3_codes")
+        w3_plane = held([P, PASSES, H], U8, "w3_plane")
+        w2_codes = held([P, PASSES, 2 * H], U8, "w2_codes")
+        w2_plane = held([P, PASSES, H], U8, "w2_plane")
+        words = {}
+
+        def gather_words(name, g0, count, home, at):
+            for a in range(PASSES):
+                c0 = (PASSES * at + a * count) * GROUP
+                cols = slice(g0 * GROUP // 16, (g0 + count) * GROUP // 16)
+                nc.vector.tensor_copy(
+                    out=home[:, c0 : c0 + count * GROUP], in_=tab[:, a, :].indirect(lists[name][:, cols])
+                )
+                for i in range(count):
+                    words[name, g0 + i, a] = home[:, c0 + i * GROUP : c0 + (i + 1) * GROUP]
+
+        def gather_a(hf):
+            gather_words("a", 2 * hf, 2, held([P, S], U32, "w1_bf%d" % hf), 0)
+
+        gather_words("c", 0, 1, held([P, PASSES * GROUP], U32, "words_c_first"), 0)
+        deal(w3_codes[:].bitcast(I32), w3_raw, 4)
+        deal(w3_plane[:].bitcast(I32), w3_plane_raw, 1)
+        words_c = held([P, PASSES * (S - GROUP)], U32, "words_c")
+        gather_words("c", 1, 1, words_c, 0)
+        gather_words("c", 2, 2, words_c, 1)
+        deal(w2_codes[:].bitcast(I32), w2_raw, 2)
+        deal(w2_plane[:].bitcast(I32), w2_plane_raw, 1)
+        words_b = held([P, PASSES * S], U32, "words_b")
+        gather_words("b", 0, 2, words_b, 0)
+        gather_words("b", 2, 2, words_b, 2)
+
+        w1_codes = [held([P, H], U32, "w1_codes%d" % a) for a in range(PASSES)]
+        w1_plane = [held([P, H], U8, "w1_plane%d" % a) for a in range(PASSES)]
+        m_codes = held([P, N], U32, "m_codes")
+        m_plane = held([P, N], U8, "m_plane")
+
+        def prepare_w1(a):
+            w1_bf = held([P, PACK * H], BF16, "w1_bf%d" % a)
+            dst = w1_bf[:].rearrange("p (t q e j) -> p t q j e", t=4, e=4, j=PACK)
+            source = w1_raw[a][:].rearrange("p j (q t e) -> p t q j e", t=4, e=4)
+            nc.scalar.copy(out=dst, in_=source)
+            nc.vector.quantize_mx(out=w1_codes[a][:].bitcast(FP8X4), scales=w1_plane[a][:], in_=w1_bf[:])
+
+        def prepare_m():
+            m_bf = held([P, PACK * N], BF16, "m_bf")
+            dst = m_bf[:].rearrange("p (u c i t) -> p u c t i", u=4, i=4, t=PACK)
+            source = m_raw[:].rearrange("p t (u c i) -> p u c t i", u=4, i=4)
+            nc.scalar.copy(out=dst, in_=source)
+            nc.vector.quantize_mx(out=m_codes[:].bitcast(FP8X4), scales=m_plane[:], in_=m_bf[:])
+
+        def stationary(name, a, t):
+            cols = slice(t * P, (t + 1) * P)
+            if name == "a":
+                return w1_codes[a][:, cols].bitcast(FP8X4), w1_plane[a][:, cols]
+            if name == "b":
+                return w2_codes[:, a, 2 * t * P : 2 * (t + 1) * P].bitcast(FP4X4), w2_plane[:, a, cols]
+            return w3_codes[:, a, cols].bitcast(FP8X4), w3_plane[:, a, cols]
+
+        def moving(name, a, g, i):
+            ch = g * PER + i
+            cols = slice(ch * CHUNK, (ch + 1) * CHUNK)
+            codes = words[name, g, a][:, i * CHUNK : (i + 1) * CHUNK].bitcast(FP8X4)
+            if name == "b" and a == 1:
+                return codes, b_plane1[:, cols]
+            return codes, planes[name][4 * a : P, cols]
+
+        def product(name, g, i, bank):
+            for t in range(PACK):
+                for a in range(PASSES):
+                    lhs, lhs_scale = stationary(name, a, t)
+                    rhs, rhs_scale = moving(name, a, g, i)
+                    nc.tensor.matmul_mx(
+                        out=bank[:, t, :], lhsT=lhs, lhsT_scale=lhs_scale, rhs=rhs, rhs_scale=rhs_scale,
+                        start=(a == 0), stop=(a == PASSES - 1),
+                    )
+            return bank[:].rearrange("p t n -> p n t")
+
+        turn = []
+
+        def next_bank():
+            turn.append(0)
+            return psum.tile([P, PACK, CHUNK], F32, name="bank%d" % ((len(turn) - 1) % 6), bufs=1)
+
+        damp = {}
+        b_sb = {}
+        h_q = {}
+
+        def stage_c(g):
+            sq = ring.tile([P, PER, WIDTH], F32, name="sq")
+            for i in range(PER):
+                bank = next_bank()
+                view = product("c", g, i, bank)
+                nc.scalar.activation(out=sq[:, i, :].rearrange("p (n t) -> p n t", t=PACK), in_=view, func=ACT.Square)
+            root = ring.tile([P, PER * WIDTH], F32, name="root")
+            nc.scalar.activation(
+                out=root[:], in_=sq[:].rearrange("p i w -> p (i w)"), func=ACT.Abs_reciprocal_sqrt, bias=1.0
+            )
+            damp[g] = held([P, PER * WIDTH], F32, "damp%d" % g)
+            nc.scalar.activation(out=damp[g][:], in_=root[:], func=ACT.Square)
+
+        def stage_b(g):
+            b_sb[g] = held([P, PER, WIDTH], F32, "b_sb%d" % g)
+            for i in range(PER):
+                bank = next_bank()
+                view = product("b", g, i, bank)
+                nc.scalar.copy(out=b_sb[g][:, i, :].rearrange("p (n t) -> p n t", t=PACK), in_=view)
+
+        diffs = {}
+
+        def stage_d(g):
+            diffs[g] = ring.tile([P, PER, WIDTH], F32, name="diff")
+            for i in range(PER):
+                bank = next_bank()
+                view = product("a", g, i, bank)
+                nc.vector.tensor_tensor(
+                    out=diffs[g][:, i, :].rearrange("p (n t) -> p n t", t=PACK),
+                    in0=view,
+                    in1=b_sb[g][:, i, :].rearrange("p (n t) -> p n t", t=PACK),
+                    op=ALU.subtract,
+                )
+
+        def stage_h(ch, count, eng):
+            g, i = divmod(ch, PER)
+            cols = slice(i * WIDTH, (i + count) * WIDTH)
+            h_bf = ring.tile([P, count * WIDTH], BF16, name="h_bf", align_bytes=64)
+            eng.tensor_tensor(
+                out=h_bf[:], in0=diffs[g][:].rearrange("p i w -> p (i w)")[:, cols], in1=damp[g][:, cols], op=ALU.mult
+            )
+            h_codes = held([P, count * CHUNK], U32, "h_codes%d" % ch)
+            h_plane = held([P, count * CHUNK], U8, "h_plane%d" % ch)
+            nc.vector.quantize_mx(out=h_codes[:].bitcast(FP8X4), scales=h_plane[:], in_=h_bf[:])
+            h_q[ch] = (h_codes, h_plane)
+
+        out_rows = out.rearrange("(t p) j -> p t j", p=P)
+
+        def stage_y(ch, count, on_vector):
+            h_codes, h_plane = h_q[ch]
+            width = count * CHUNK
+            y_sb = held([P, N // P, width], F32, "y_sb%d" % ch)
+            per_bank = 512 // width
+            for first in range(0, N // P, per_bank):
+                ybank = next_bank() if on_vector else psum.tile([P, per_bank, width], F32, name="ybank")
+                for u in range(per_bank):
+                    cols = slice((first + u) * P, (first + u + 1) * P)
+                    nc.tensor.matmul_mx(
+                        out=ybank[:, u, :], lhsT=m_codes[:, cols].bitcast(FP8X4), lhsT_scale=m_plane[:, cols],
+                        rhs=h_codes[:].bitcast(FP8X4), rhs_scale=h_plane[:], start=True, stop=True,
+                    )
+                if on_vector:
+                    nc.vector.tensor_tensor(
+                        out=y_sb[:, first : first + per_bank, :],
+                        in0=ybank[:],
+                        in1=src_col[:, first : first + per_bank].unsqueeze(2).to_broadcast([P, per_bank, width]),
+                        op=ALU.add,
+                    )
+                else:
+                    for u in range(per_bank):
+                        nt = first + u
+                        nc.scalar.activation(
+                            out=y_sb[:, nt, :], in_=ybank[:, u, :], func=ACT.Identity, bias=src_col[:, nt : nt + 1]
+                        )
+            nc.sync.dma_start(out=out_rows[:, :, ch * CHUNK : ch * CHUNK + width], in_=y_sb[:])
+
+        stage_c(0)
+        prepare_w1(0)
+        gather_plane("a", "w1_raw0")
+        gather_a(0)
+        prepare_w1(1)
+        gather_a(1)
+        stage_c(1)
+        stage_b(0)
+        stage_c(2)
+        stage_b(1)
+        stage_d(0)
+        stage_h(0, 2, nc.vector)
+        stage_b(2)
+        prepare_m()
+        stage_d(1)
+        stage_h(2, 2, nc.vector)
+        stage_c(3)
+        stage_b(3)
+        stage_d(2)
+        stage_h(4, 2, nc.vector)
+        stage_d(3)
+        stage_h(6, 1, nc.vector)
+        stage_h(7, 1, nc.vector)
+        stage_y(0, 2, False)
+        stage_y(2, 2, False)
+        stage_y(4, 2, False)
+        stage_y(6, 1, True)
+        stage_y(7, 1, True)

@@ -18,13 +18,19 @@ ALU = mybir.AluOpType
 
 P = 128
 PACK = 4
-PASSES = K // (P * PACK)
+PASS_K = P * PACK
+PASSES = K // PASS_K
 QUADS = 4
+ROWS = 4
+RUN = 4
+PER_COLUMN = 16
 CHUNK = 128
-GROUP = 256
+BANK = PACK * CHUNK
+PER = 2
+GROUP = PER * CHUNK
 GROUPS = S // GROUP
-PER = GROUP // CHUNK
-WIDTH = PACK * CHUNK
+N_TILES = N // P
+RING_BANKS = {"scalar": 4, "vector": 2, "spare": 2}
 
 
 def tile_list_damped_mesh_flux_kernel(
@@ -34,33 +40,34 @@ def tile_list_damped_mesh_flux_kernel(
     with ExitStack() as ctx:
         keep = ctx.enter_context(tc.tile_pool(name="keep", bufs=1))
         ring = ctx.enter_context(tc.tile_pool(name="ring", bufs=2))
-        psum = ctx.enter_context(tc.psum_pool(name="psum", bufs=2))
+        psum = ctx.enter_context(tc.psum_pool(name="psum", bufs=1))
 
         def held(shape, dtype, name):
             return keep.tile(shape, dtype, name=name, align_bytes=64)
 
-        lists = {name: held([P, S // 16], U16, "list_" + name) for name in "cba"}
+        lists = {name: held([P, S // PER_COLUMN], U16, "list_" + name) for name in "cba"}
 
         tab_plane = held([P, T], U8, "tab_plane")
         nc.vector.memset(tab_plane[:].bitcast(I32), 0)
-        w3_stage = held([P, PASSES * (H + H // 4)], I32, "words_c")
-        w2_stage = held([P, PASSES * (H // 2 + H // 4)], I32, "words_b")
-        w3_raw = w3_stage[:, : PASSES * H].rearrange("p (a e) -> p a e", a=PASSES)
-        w3_plane_raw = w3_stage[:, PASSES * H :].rearrange("p (a e) -> p a e", a=PASSES)
-        w2_raw = w2_stage[:, : PASSES * H // 2].rearrange("p (a e) -> p a e", a=PASSES)
-        w2_plane_raw = w2_stage[:, PASSES * H // 2 :].rearrange("p (a e) -> p a e", a=PASSES)
-        b_plane1 = held([P, S], U8, "b_plane1")
-        nc.vector.memset(w3_stage[:, PASSES * H :], 0)
-        nc.vector.memset(w2_stage[:, PASSES * H // 2 :], 0)
-        nc.gpsimd.memset(b_plane1[:].bitcast(I32), 0)
+        w3_ints, w2_ints, plane_ints = H, H // 2, H // 4
+        w3_stage = held([P, PASSES * (w3_ints + plane_ints)], I32, "words_c")
+        w2_stage = held([P, PASSES * (w2_ints + plane_ints)], I32, "words_b")
+        w3_raw = w3_stage[:, : PASSES * w3_ints].rearrange("p (a e) -> p a e", a=PASSES)
+        w3_plane_raw = w3_stage[:, PASSES * w3_ints :].rearrange("p (a e) -> p a e", a=PASSES)
+        w2_raw = w2_stage[:, : PASSES * w2_ints].rearrange("p (a e) -> p a e", a=PASSES)
+        w2_plane_raw = w2_stage[:, PASSES * w2_ints :].rearrange("p (a e) -> p a e", a=PASSES)
+        b_plane_pass1 = held([P, S], U8, "b_plane_pass1")
+        nc.vector.memset(w3_stage[:, PASSES * w3_ints :], 0)
+        nc.vector.memset(w2_stage[:, PASSES * w2_ints :], 0)
+        nc.gpsimd.memset(b_plane_pass1[:].bitcast(I32), 0)
 
         nc.sync.dma_start(lists["c"][:], offs3)
         nc.sync.dma_start(lists["b"][:], offs2)
         nc.sync.dma_start(lists["a"][:], offs)
         for q in range(QUADS):
             nc.sync.dma_start(
-                out=tab_plane[32 * q : 32 * q + 8, :].bitcast(I32),
-                in_=tab_scales[:, 4 * q : 4 * q + 4, :].bitcast(I32),
+                out=tab_plane[32 * q : 32 * q + PASSES * ROWS, :].bitcast(I32),
+                in_=tab_scales[:, ROWS * q : ROWS * (q + 1), :].bitcast(I32),
             )
         tab = held([P, PASSES, T], U32, "tab")
         nc.sync.dma_start(out=tab[:].bitcast(I32), in_=tab_words.rearrange("a p t i -> p a (t i)").bitcast(I32))
@@ -68,77 +75,75 @@ def tile_list_damped_mesh_flux_kernel(
         def load_plane(raw, scales):
             for q in range(QUADS):
                 nc.sync.dma_start(
-                    out=raw[32 * q : 32 * q + 4, :, :],
-                    in_=scales[:, 4 * q : 4 * q + 4, :].rearrange("a r e -> r a e").bitcast(I32),
+                    out=raw[32 * q : 32 * q + ROWS, :, :],
+                    in_=scales[:, ROWS * q : ROWS * (q + 1), :].rearrange("a r e -> r a e").bitcast(I32),
                 )
 
         nc.sync.dma_start(out=w3_raw, in_=w3_words.rearrange("a p e i -> p a (e i)").bitcast(I32))
         load_plane(w3_plane_raw, w3_scales)
         nc.sync.dma_start(out=w2_raw, in_=w2_words.rearrange("a p e -> p a e").bitcast(I32))
-        load_plane(w2_plane_raw, w2_scales)
-        w1_raw = []
+        w1_raw = [held([P, PACK, H], F32, "w1_raw%d" % a) for a in range(PASSES)]
         for a in range(PASSES):
-            raw = held([P, PACK, H], F32, "w1_raw%d" % a)
-            nc.sync.dma_start(out=raw[:], in_=w1[512 * a : 512 * (a + 1), :].rearrange("(p j) c -> p j c", j=PACK))
-            w1_raw.append(raw)
+            rows = w1[PASS_K * a : PASS_K * (a + 1), :].rearrange("(p j) c -> p j c", j=PACK)
+            nc.sync.dma_start(out=w1_raw[a][:], in_=rows)
+        load_plane(w2_plane_raw, w2_scales)
 
         planes = {}
+        words = {}
 
-        def gather_plane(name, tag):
-            planes[name] = held([P, S], U8, tag)
+        def gather_plane(name, home):
+            planes[name] = held([P, S], U8, home)
             nc.vector.tensor_copy(out=planes[name][:], in_=tab_plane[:].indirect(lists[name][:]))
+
+        def gather_words(name, first, count, home):
+            cols = slice(first * GROUP // PER_COLUMN, (first + count) * GROUP // PER_COLUMN)
+            for a in range(PASSES):
+                dst = home[:, a * count * GROUP : (a + 1) * count * GROUP]
+                nc.vector.tensor_copy(out=dst, in_=tab[:, a, :].indirect(lists[name][:, cols]))
+                for i in range(count):
+                    words[name, first + i, a] = dst[:, i * GROUP : (i + 1) * GROUP]
 
         gather_plane("c", "plane_c")
         gather_plane("b", "plane_b")
         for q in range(QUADS):
             nc.sync.dma_start(
-                out=b_plane1[32 * q : 32 * q + 4, :].bitcast(I32),
-                in_=planes["b"][32 * q + 4 : 32 * q + 8, :].bitcast(I32),
+                out=b_plane_pass1[32 * q : 32 * q + ROWS, :].bitcast(I32),
+                in_=planes["b"][32 * q + ROWS : 32 * q + 2 * ROWS, :].bitcast(I32),
             )
         m_raw = held([P, PACK, N], F32, "m_raw")
-        m_rows = m.rearrange("(q t e) n -> e q t n", t=4, e=4)
-        for e in range(4):
-            nc.sync.dma_start(out=m_raw[e:P:4, :, :], in_=m_rows[e])
-        src_col = held([P, N // P], F32, "src_col")
+        m_rows = m.rearrange("(q t e) n -> t q e n", t=PACK, e=RUN)
+        for t in range(PACK):
+            nc.sync.dma_start(out=m_raw[:, t, :], in_=m_rows[t])
+        src_col = held([P, N_TILES], F32, "src_col")
         with nc.allow_non_contiguous_dma(reason="one source value for each partition and output tile"):
             nc.sync.dma_start(out=src_col[:], in_=src.rearrange("(t p) -> p t", p=P))
 
-        def deal(dst, source, run):
+        def deal(dst, source, ints):
             nc.vector.tensor_copy(
-                out=dst.rearrange("p a (t q e) -> p a t q e", t=4, e=run),
-                in_=source.rearrange("p a (q t e) -> p a t q e", t=4, e=run),
+                out=dst.rearrange("p a (t q e) -> p a q t e", t=PACK, e=ints),
+                in_=source.rearrange("p a (q t e) -> p a q t e", t=PACK, e=ints),
             )
 
         w3_codes = held([P, PASSES, H], U32, "w3_codes")
         w3_plane = held([P, PASSES, H], U8, "w3_plane")
         w2_codes = held([P, PASSES, 2 * H], U8, "w2_codes")
         w2_plane = held([P, PASSES, H], U8, "w2_plane")
-        words = {}
 
-        def gather_words(name, g0, count, home, at):
-            for a in range(PASSES):
-                c0 = (PASSES * at + a * count) * GROUP
-                cols = slice(g0 * GROUP // 16, (g0 + count) * GROUP // 16)
-                nc.vector.tensor_copy(
-                    out=home[:, c0 : c0 + count * GROUP], in_=tab[:, a, :].indirect(lists[name][:, cols])
-                )
-                for i in range(count):
-                    words[name, g0 + i, a] = home[:, c0 + i * GROUP : c0 + (i + 1) * GROUP]
-
-        def gather_a(hf):
-            gather_words("a", 2 * hf, 2, held([P, S], U32, "w1_bf%d" % hf), 0)
-
-        gather_words("c", 0, 1, held([P, PASSES * GROUP], U32, "words_c_first"), 0)
-        deal(w3_codes[:].bitcast(I32), w3_raw, 4)
-        deal(w3_plane[:].bitcast(I32), w3_plane_raw, 1)
+        gather_words("c", 0, 1, held([P, PASSES * GROUP], U32, "words_c_first"))
+        deal(w3_codes[:].bitcast(I32), w3_raw, RUN * w3_ints // H)
+        deal(w3_plane[:].bitcast(I32), w3_plane_raw, RUN * plane_ints // H)
         words_c = held([P, PASSES * (S - GROUP)], U32, "words_c")
-        gather_words("c", 1, 1, words_c, 0)
-        gather_words("c", 2, 2, words_c, 1)
-        deal(w2_codes[:].bitcast(I32), w2_raw, 2)
-        deal(w2_plane[:].bitcast(I32), w2_plane_raw, 1)
-        words_b = held([P, PASSES * S], U32, "words_b")
-        gather_words("b", 0, 2, words_b, 0)
-        gather_words("b", 2, 2, words_b, 2)
+        gather_words("c", 1, 1, words_c[:, : PASSES * GROUP])
+        gather_words("c", 2, 2, words_c[:, PASSES * GROUP :])
+        deal(w2_codes[:].bitcast(I32), w2_raw, RUN * w2_ints // H)
+
+        def gather_after_first_c():
+            gather_plane("a", "words_c_first")
+            deal(w2_plane[:].bitcast(I32), w2_plane_raw, RUN * plane_ints // H)
+            words_b = held([P, PASSES * S], U32, "words_b")
+            half = GROUPS // 2
+            gather_words("b", 0, half, words_b[:, :S])
+            gather_words("b", half, half, words_b[:, S:])
 
         w1_codes = [held([P, H], U32, "w1_codes%d" % a) for a in range(PASSES)]
         w1_plane = [held([P, H], U8, "w1_plane%d" % a) for a in range(PASSES)]
@@ -147,17 +152,28 @@ def tile_list_damped_mesh_flux_kernel(
 
         def prepare_w1(a):
             w1_bf = held([P, PACK * H], BF16, "w1_bf%d" % a)
-            dst = w1_bf[:].rearrange("p (t q e j) -> p t q j e", t=4, e=4, j=PACK)
-            source = w1_raw[a][:].rearrange("p j (q t e) -> p t q j e", t=4, e=4)
-            nc.scalar.copy(out=dst, in_=source)
+            nc.scalar.copy(
+                out=w1_bf[:].rearrange("p (t q e j) -> p t q j e", t=PACK, e=RUN, j=PACK),
+                in_=w1_raw[a][:].rearrange("p j (q t e) -> p t q j e", t=PACK, e=RUN),
+            )
             nc.vector.quantize_mx(out=w1_codes[a][:].bitcast(FP8X4), scales=w1_plane[a][:], in_=w1_bf[:])
+            half = GROUPS // PASSES
+            gather_words("a", a * half, half, held([P, S], U32, "w1_bf%d" % a))
 
         def prepare_m():
             m_bf = held([P, PACK * N], BF16, "m_bf")
-            dst = m_bf[:].rearrange("p (u c i t) -> p u c t i", u=4, i=4, t=PACK)
-            source = m_raw[:].rearrange("p t (u c i) -> p u c t i", u=4, i=4)
-            nc.scalar.copy(out=dst, in_=source)
+            nc.scalar.copy(
+                out=m_bf[:].rearrange("p (c i t) -> p c t i", i=RUN, t=PACK),
+                in_=m_raw[:].rearrange("p t (c i) -> p c t i", i=RUN),
+            )
             nc.vector.quantize_mx(out=m_codes[:].bitcast(FP8X4), scales=m_plane[:], in_=m_bf[:])
+
+        taken = {which: [] for which in RING_BANKS}
+
+        def next_bank(which):
+            turn = len(taken[which]) % RING_BANKS[which]
+            taken[which].append(turn)
+            return psum.tile([P, PACK, CHUNK], F32, name="%s%d" % (which, turn))
 
         def stationary(name, a, t):
             cols = slice(t * P, (t + 1) * P)
@@ -168,135 +184,145 @@ def tile_list_damped_mesh_flux_kernel(
             return w3_codes[:, a, cols].bitcast(FP8X4), w3_plane[:, a, cols]
 
         def moving(name, a, g, i):
-            ch = g * PER + i
-            cols = slice(ch * CHUNK, (ch + 1) * CHUNK)
+            cols = slice(g * GROUP + i * CHUNK, g * GROUP + (i + 1) * CHUNK)
             codes = words[name, g, a][:, i * CHUNK : (i + 1) * CHUNK].bitcast(FP8X4)
             if name == "b" and a == 1:
-                return codes, b_plane1[:, cols]
-            return codes, planes[name][4 * a : P, cols]
+                return codes, b_plane_pass1[:, cols]
+            return codes, planes[name][ROWS * a : P, cols]
 
-        def product(name, g, i, bank):
-            for t in range(PACK):
-                for a in range(PASSES):
-                    lhs, lhs_scale = stationary(name, a, t)
-                    rhs, rhs_scale = moving(name, a, g, i)
-                    nc.tensor.matmul_mx(
-                        out=bank[:, t, :], lhsT=lhs, lhsT_scale=lhs_scale, rhs=rhs, rhs_scale=rhs_scale,
-                        start=(a == 0), stop=(a == PASSES - 1),
-                    )
-            return bank[:].rearrange("p t n -> p n t")
+        sums = {}
 
-        turn = []
-
-        def next_bank():
-            turn.append(0)
-            return psum.tile([P, PACK, CHUNK], F32, name="bank%d" % ((len(turn) - 1) % 6), bufs=1)
-
-        damp = {}
-        b_sb = {}
-        h_q = {}
-
-        def stage_c(g):
-            sq = ring.tile([P, PER, WIDTH], F32, name="sq")
+        def product(name, g, which):
             for i in range(PER):
-                bank = next_bank()
-                view = product("c", g, i, bank)
-                nc.scalar.activation(out=sq[:, i, :].rearrange("p (n t) -> p n t", t=PACK), in_=view, func=ACT.Square)
-            root = ring.tile([P, PER * WIDTH], F32, name="root")
-            nc.scalar.activation(
-                out=root[:], in_=sq[:].rearrange("p i w -> p (i w)"), func=ACT.Abs_reciprocal_sqrt, bias=1.0
-            )
-            damp[g] = held([P, PER * WIDTH], F32, "damp%d" % g)
-            nc.scalar.activation(out=damp[g][:], in_=root[:], func=ACT.Square)
+                bank = next_bank(which)
+                for t in range(PACK):
+                    for a in range(PASSES):
+                        lhs, lhs_scale = stationary(name, a, t)
+                        rhs, rhs_scale = moving(name, a, g, i)
+                        nc.tensor.matmul_mx(
+                            out=bank[:, t, :], lhsT=lhs, lhsT_scale=lhs_scale, rhs=rhs, rhs_scale=rhs_scale,
+                            start=(a == 0), stop=(a == PASSES - 1),
+                        )
+                sums[name, g, i] = bank[:].rearrange("p t n -> p n t")
 
-        def stage_b(g):
-            b_sb[g] = held([P, PER, WIDTH], F32, "b_sb%d" % g)
+        def chunk_of(tile, i):
+            return tile[:, i * BANK : (i + 1) * BANK].rearrange("p (n t) -> p n t", t=PACK)
+
+        root, damp, b_kept, diff, h_mx = {}, {}, {}, {}, {}
+
+        def inverse_root(g):
+            square = ring.tile([P, PER * BANK], F32, name="square")
             for i in range(PER):
-                bank = next_bank()
-                view = product("b", g, i, bank)
-                nc.scalar.copy(out=b_sb[g][:, i, :].rearrange("p (n t) -> p n t", t=PACK), in_=view)
+                nc.scalar.activation(out=chunk_of(square, i), in_=sums["c", g, i], func=ACT.Square)
+            root[g] = ring.tile([P, PER * BANK], F32, name="root")
+            nc.scalar.activation(out=root[g][:], in_=square[:], func=ACT.Abs_reciprocal_sqrt, bias=1.0)
 
-        diffs = {}
+        def damping(g):
+            damp[g] = held([P, PER * BANK], F32, "damp%d" % g)
+            nc.scalar.activation(out=damp[g][:], in_=root[g][:], func=ACT.Square)
 
-        def stage_d(g):
-            diffs[g] = ring.tile([P, PER, WIDTH], F32, name="diff")
+        def keep_b(g):
+            b_kept[g] = held([P, PER * BANK], F32, "b_kept%d" % g)
             for i in range(PER):
-                bank = next_bank()
-                view = product("a", g, i, bank)
+                nc.scalar.copy(out=chunk_of(b_kept[g], i), in_=sums["b", g, i])
+
+        def difference(g):
+            diff[g] = held([P, PER * BANK], F32, "diff%d" % g)
+            for i in range(PER):
                 nc.vector.tensor_tensor(
-                    out=diffs[g][:, i, :].rearrange("p (n t) -> p n t", t=PACK),
-                    in0=view,
-                    in1=b_sb[g][:, i, :].rearrange("p (n t) -> p n t", t=PACK),
-                    op=ALU.subtract,
+                    out=chunk_of(diff[g], i), in0=sums["a", g, i], in1=chunk_of(b_kept[g], i), op=ALU.subtract
                 )
 
-        def stage_h(ch, count, eng):
-            g, i = divmod(ch, PER)
-            cols = slice(i * WIDTH, (i + count) * WIDTH)
-            h_bf = ring.tile([P, count * WIDTH], BF16, name="h_bf", align_bytes=64)
-            eng.tensor_tensor(
-                out=h_bf[:], in0=diffs[g][:].rearrange("p i w -> p (i w)")[:, cols], in1=damp[g][:, cols], op=ALU.mult
-            )
-            h_codes = held([P, count * CHUNK], U32, "h_codes%d" % ch)
-            h_plane = held([P, count * CHUNK], U8, "h_plane%d" % ch)
-            nc.vector.quantize_mx(out=h_codes[:].bitcast(FP8X4), scales=h_plane[:], in_=h_bf[:])
-            h_q[ch] = (h_codes, h_plane)
+        def flux(piece):
+            g, i, count = piece
+            cols = slice(i * BANK, (i + count) * BANK)
+            h_bf = ring.tile([P, count * BANK], BF16, name="h_bf", align_bytes=64)
+            nc.vector.tensor_tensor(out=h_bf[:], in0=diff[g][:, cols], in1=damp[g][:, cols], op=ALU.mult)
+            codes = held([P, count * CHUNK], U32, "h_codes%d_%d" % (g, i))
+            plane = held([P, count * CHUNK], U8, "h_plane%d_%d" % (g, i))
+            nc.vector.quantize_mx(out=codes[:].bitcast(FP8X4), scales=plane[:], in_=h_bf[:])
+            h_mx[piece] = (codes, plane)
 
-        out_rows = out.rearrange("(t p) j -> p t j", p=P)
+        out_rows = out.rearrange("(u p) j -> p u j", p=P)
+        updates = {}
 
-        def stage_y(ch, count, on_vector):
-            h_codes, h_plane = h_q[ch]
-            width = count * CHUNK
-            y_sb = held([P, N // P, width], F32, "y_sb%d" % ch)
-            per_bank = 512 // width
-            for first in range(0, N // P, per_bank):
-                ybank = next_bank() if on_vector else psum.tile([P, per_bank, width], F32, name="ybank")
+        def update(piece, which):
+            codes, plane = h_mx[piece]
+            per_bank = PACK // piece[2]
+            updates[piece] = []
+            for first in range(0, N_TILES, per_bank):
+                bank = next_bank(which)[:].rearrange("p t n -> p (t n)").rearrange("p (u w) -> p u w", u=per_bank)
                 for u in range(per_bank):
                     cols = slice((first + u) * P, (first + u + 1) * P)
                     nc.tensor.matmul_mx(
-                        out=ybank[:, u, :], lhsT=m_codes[:, cols].bitcast(FP8X4), lhsT_scale=m_plane[:, cols],
-                        rhs=h_codes[:].bitcast(FP8X4), rhs_scale=h_plane[:], start=True, stop=True,
+                        out=bank[:, u, :], lhsT=m_codes[:, cols].bitcast(FP8X4), lhsT_scale=m_plane[:, cols],
+                        rhs=codes[:].bitcast(FP8X4), rhs_scale=plane[:], start=True, stop=True,
                     )
+                updates[piece].append((first, bank))
+
+        def store(piece, on_vector):
+            g, i, count = piece
+            per_bank, width, start = PACK // count, count * CHUNK, g * GROUP + i * CHUNK
+            for first, bank in updates[piece]:
+                result = held([P, per_bank, width], F32, "result%d_%d_%d" % (g, i, first))
                 if on_vector:
-                    nc.vector.tensor_tensor(
-                        out=y_sb[:, first : first + per_bank, :],
-                        in0=ybank[:],
-                        in1=src_col[:, first : first + per_bank].unsqueeze(2).to_broadcast([P, per_bank, width]),
-                        op=ALU.add,
-                    )
+                    spread = src_col[:, first : first + per_bank].unsqueeze(2).to_broadcast([P, per_bank, width])
+                    nc.vector.tensor_tensor(out=result[:], in0=bank, in1=spread, op=ALU.add)
                 else:
                     for u in range(per_bank):
-                        nt = first + u
                         nc.scalar.activation(
-                            out=y_sb[:, nt, :], in_=ybank[:, u, :], func=ACT.Identity, bias=src_col[:, nt : nt + 1]
+                            out=result[:, u, :], in_=bank[:, u, :], func=ACT.Identity,
+                            bias=src_col[:, first + u : first + u + 1],
                         )
-            nc.sync.dma_start(out=out_rows[:, :, ch * CHUNK : ch * CHUNK + width], in_=y_sb[:])
+                nc.sync.dma_start(out=out_rows[:, first : first + per_bank, start : start + width], in_=result[:])
 
-        stage_c(0)
-        prepare_w1(0)
-        gather_plane("a", "w1_raw0")
-        gather_a(0)
-        prepare_w1(1)
-        gather_a(1)
-        stage_c(1)
-        stage_b(0)
-        stage_c(2)
-        stage_b(1)
-        stage_d(0)
-        stage_h(0, 2, nc.vector)
-        stage_b(2)
+        early, late = range(GROUPS // 2), range(GROUPS // 2, GROUPS)
+        whole = [(g, 0, PER) for g in range(GROUPS - 1)]
+        last = [(GROUPS - 1, i, 1) for i in range(PER)]
+
+        product("c", 0, "scalar")
+        gather_after_first_c()
+        product("c", 1, "scalar")
+        product("b", 0, "scalar")
+        product("b", 1, "vector")
+        product("c", late[0], "scalar")
+        for g in early:
+            inverse_root(g)
+            damping(g)
+        for a in range(PASSES):
+            prepare_w1(a)
+        keep_b(0)
+        product("b", late[0], "scalar")
+        product("b", late[1], "spare")
+        keep_b(1)
+        product("a", 0, "vector")
         prepare_m()
-        stage_d(1)
-        stage_h(2, 2, nc.vector)
-        stage_c(3)
-        stage_b(3)
-        stage_d(2)
-        stage_h(4, 2, nc.vector)
-        stage_d(3)
-        stage_h(6, 1, nc.vector)
-        stage_h(7, 1, nc.vector)
-        stage_y(0, 2, False)
-        stage_y(2, 2, False)
-        stage_y(4, 2, False)
-        stage_y(6, 1, True)
-        stage_y(7, 1, True)
+        for g in early:
+            difference(g)
+            product("a", g + 1, "vector")
+            flux(whole[g])
+
+        inverse_root(late[0])
+        product("c", late[1], "scalar")
+        keep_b(late[0])
+        update(whole[0], "scalar")
+        damping(late[0])
+        inverse_root(late[1])
+        update(whole[1], "scalar")
+        keep_b(late[1])
+        store(whole[0], on_vector=False)
+        damping(late[1])
+
+        difference(late[0])
+        product("a", late[1], "vector")
+        flux(whole[late[0]])
+        update(whole[late[0]], "spare")
+        store(whole[1], on_vector=False)
+        difference(late[1])
+        for piece in last:
+            flux(piece)
+        for piece in last:
+            update(piece, "scalar")
+        store(whole[late[0]], on_vector=False)
+        store(last[0], on_vector=False)
+        store(last[1], on_vector=True)

@@ -162,10 +162,10 @@ def tile_list_damped_mesh_flux_kernel(
 
         def prepare_m():
             m_bf = held([P, PACK * N], BF16, "m_bf")
-            nc.scalar.copy(
-                out=m_bf[:].rearrange("p (c i t) -> p c t i", i=RUN, t=PACK),
-                in_=m_raw[:].rearrange("p t (c i) -> p c t i", i=RUN),
-            )
+            dst = m_bf[:].rearrange("p (half c i t) -> p half c t i", half=2, i=RUN, t=PACK)
+            source = m_raw[:].rearrange("p t (half c i) -> p half c t i", half=2, i=RUN)
+            nc.scalar.copy(out=dst[:, 0], in_=source[:, 0])
+            nc.vector.tensor_copy(out=dst[:, 1], in_=source[:, 1])
             nc.vector.quantize_mx(out=m_codes[:].bitcast(FP8X4), scales=m_plane[:], in_=m_bf[:])
 
         taken = {which: [] for which in RING_BANKS}
@@ -324,5 +324,5 @@ def tile_list_damped_mesh_flux_kernel(
         for piece in last:
             update(piece, "scalar")
         store(whole[late[0]], on_vector=False)
-        store(last[0], on_vector=False)
-        store(last[1], on_vector=True)
+        for piece in last:
+            store(piece, on_vector=True)

from contextlib import ExitStack

import concourse.mybir as mybir

K, H, N, T, S = 1024, 512, 512, 2048, 1024
FLOPS = 2 * (3 * K * H * S + H * N * S)

F32 = mybir.dt.float32
BF16 = mybir.dt.bfloat16
I32 = mybir.dt.int32
U32 = mybir.dt.uint32
U16 = mybir.dt.uint16
U8 = mybir.dt.uint8
FP8X4 = mybir.dt.float8_e4m3fn_x4
FP4X4 = mybir.dt.float4_e2m1fn_x4
ACT = mybir.ActivationFunctionType
ALU = mybir.AluOpType

P = 128
PACK = 4
PASS_K = P * PACK
PASSES = K // PASS_K
QUADS = 4
ROWS = 4
RUN = 4
PER_COLUMN = 16
CHUNK = 128
BANK = PACK * CHUNK
PER = 2
GROUP = PER * CHUNK
GROUPS = S // GROUP
N_TILES = N // P
RING_BANKS = {"scalar": 4, "vector": 2, "spare": 2}


def tile_list_damped_mesh_flux_kernel(
    tc, tab_words, tab_scales, offs, offs2, offs3, w1, w2_words, w2_scales, w3_words, w3_scales, m, src, out
):
    nc = tc.nc
    with ExitStack() as ctx:
        keep = ctx.enter_context(tc.tile_pool(name="keep", bufs=1))
        ring = ctx.enter_context(tc.tile_pool(name="ring", bufs=2))
        psum = ctx.enter_context(tc.psum_pool(name="psum", bufs=1))

        def held(shape, dtype, name):
            return keep.tile(shape, dtype, name=name, align_bytes=64)

        lists = {name: held([P, S // PER_COLUMN], U16, "list_" + name) for name in "cba"}

        tab_plane = held([P, T], U8, "tab_plane")
        nc.vector.memset(tab_plane[:].bitcast(I32), 0)
        w3_ints, w2_ints, plane_ints = H, H // 2, H // 4
        w3_stage = held([P, PASSES * (w3_ints + plane_ints)], I32, "words_c")
        w2_stage = held([P, PASSES * (w2_ints + plane_ints)], I32, "words_b")
        w3_raw = w3_stage[:, : PASSES * w3_ints].rearrange("p (a e) -> p a e", a=PASSES)
        w3_plane_raw = w3_stage[:, PASSES * w3_ints :].rearrange("p (a e) -> p a e", a=PASSES)
        w2_raw = w2_stage[:, : PASSES * w2_ints].rearrange("p (a e) -> p a e", a=PASSES)
        w2_plane_raw = w2_stage[:, PASSES * w2_ints :].rearrange("p (a e) -> p a e", a=PASSES)
        b_plane_pass1 = held([P, S], U8, "b_plane_pass1")
        nc.vector.memset(w3_stage[:, PASSES * w3_ints :], 0)
        nc.vector.memset(w2_stage[:, PASSES * w2_ints :], 0)
        nc.gpsimd.memset(b_plane_pass1[:].bitcast(I32), 0)

        nc.sync.dma_start(lists["c"][:], offs3)
        nc.sync.dma_start(lists["b"][:], offs2)
        nc.sync.dma_start(lists["a"][:], offs)
        for q in range(QUADS):
            nc.sync.dma_start(
                out=tab_plane[32 * q : 32 * q + PASSES * ROWS, :].bitcast(I32),
                in_=tab_scales[:, ROWS * q : ROWS * (q + 1), :].bitcast(I32),
            )
        tab = held([P, PASSES, T], U32, "tab")
        nc.sync.dma_start(out=tab[:].bitcast(I32), in_=tab_words.rearrange("a p t i -> p a (t i)").bitcast(I32))

        def load_plane(raw, scales):
            for q in range(QUADS):
                nc.sync.dma_start(
                    out=raw[32 * q : 32 * q + ROWS, :, :],
                    in_=scales[:, ROWS * q : ROWS * (q + 1), :].rearrange("a r e -> r a e").bitcast(I32),
                )

        nc.sync.dma_start(out=w3_raw, in_=w3_words.rearrange("a p e i -> p a (e i)").bitcast(I32))
        load_plane(w3_plane_raw, w3_scales)
        nc.sync.dma_start(out=w2_raw, in_=w2_words.rearrange("a p e -> p a e").bitcast(I32))
        w1_raw = [held([P, PACK, H], F32, "w1_raw%d" % a) for a in range(PASSES)]
        for a in range(PASSES):
            rows = w1[PASS_K * a : PASS_K * (a + 1), :].rearrange("(p j) c -> p j c", j=PACK)
            nc.sync.dma_start(out=w1_raw[a][:], in_=rows)
        load_plane(w2_plane_raw, w2_scales)

        planes = {}
        words = {}

        def gather_plane(name, home):
            planes[name] = held([P, S], U8, home)
            nc.vector.tensor_copy(out=planes[name][:], in_=tab_plane[:].indirect(lists[name][:]))

        def gather_words(name, first, count, home):
            cols = slice(first * GROUP // PER_COLUMN, (first + count) * GROUP // PER_COLUMN)
            for a in range(PASSES):
                dst = home[:, a * count * GROUP : (a + 1) * count * GROUP]
                nc.vector.tensor_copy(out=dst, in_=tab[:, a, :].indirect(lists[name][:, cols]))
                for i in range(count):
                    words[name, first + i, a] = dst[:, i * GROUP : (i + 1) * GROUP]

        gather_plane("c", "plane_c")
        gather_plane("b", "plane_b")
        for q in range(QUADS):
            nc.sync.dma_start(
                out=b_plane_pass1[32 * q : 32 * q + ROWS, :].bitcast(I32),
                in_=planes["b"][32 * q + ROWS : 32 * q + 2 * ROWS, :].bitcast(I32),
            )
        m_raw = held([P, PACK, N], F32, "m_raw")
        m_rows = m.rearrange("(q t e) n -> t q e n", t=PACK, e=RUN)
        for t in range(PACK):
            nc.sync.dma_start(out=m_raw[:, t, :], in_=m_rows[t])
        src_col = held([P, N_TILES], F32, "src_col")
        with nc.allow_non_contiguous_dma(reason="one source value for each partition and output tile"):
            nc.sync.dma_start(out=src_col[:], in_=src.rearrange("(t p) -> p t", p=P))

        def deal(dst, source, ints):
            nc.vector.tensor_copy(
                out=dst.rearrange("p a (t q e) -> p a q t e", t=PACK, e=ints),
                in_=source.rearrange("p a (q t e) -> p a q t e", t=PACK, e=ints),
            )

        w3_codes = held([P, PASSES, H], U32, "w3_codes")
        w3_plane = held([P, PASSES, H], U8, "w3_plane")
        w2_codes = held([P, PASSES, 2 * H], U8, "w2_codes")
        w2_plane = held([P, PASSES, H], U8, "w2_plane")

        gather_words("c", 0, 1, held([P, PASSES * GROUP], U32, "words_c_first"))
        deal(w3_codes[:].bitcast(I32), w3_raw, RUN * w3_ints // H)
        deal(w3_plane[:].bitcast(I32), w3_plane_raw, RUN * plane_ints // H)
        words_c = held([P, PASSES * (S - GROUP)], U32, "words_c")
        gather_words("c", 1, 1, words_c[:, : PASSES * GROUP])
        gather_words("c", 2, 2, words_c[:, PASSES * GROUP :])
        deal(w2_codes[:].bitcast(I32), w2_raw, RUN * w2_ints // H)

        def gather_after_first_c():
            gather_plane("a", "words_c_first")
            deal(w2_plane[:].bitcast(I32), w2_plane_raw, RUN * plane_ints // H)
            words_b = held([P, PASSES * S], U32, "words_b")
            half = GROUPS // 2
            gather_words("b", 0, half, words_b[:, :S])
            gather_words("b", half, half, words_b[:, S:])

        w1_codes = [held([P, H], U32, "w1_codes%d" % a) for a in range(PASSES)]
        w1_plane = [held([P, H], U8, "w1_plane%d" % a) for a in range(PASSES)]
        m_codes = held([P, N], U32, "m_codes")
        m_plane = held([P, N], U8, "m_plane")

        def prepare_w1(a):
            w1_bf = held([P, PACK * H], BF16, "w1_bf%d" % a)
            nc.scalar.copy(
                out=w1_bf[:].rearrange("p (t q e j) -> p t q j e", t=PACK, e=RUN, j=PACK),
                in_=w1_raw[a][:].rearrange("p j (q t e) -> p t q j e", t=PACK, e=RUN),
            )
            nc.vector.quantize_mx(out=w1_codes[a][:].bitcast(FP8X4), scales=w1_plane[a][:], in_=w1_bf[:])
            half = GROUPS // PASSES
            gather_words("a", a * half, half, held([P, S], U32, "w1_bf%d" % a))

        def prepare_m():
            m_bf = held([P, PACK * N], BF16, "m_bf")
            dst = m_bf[:].rearrange("p (half c i t) -> p half c t i", half=2, i=RUN, t=PACK)
            source = m_raw[:].rearrange("p t (half c i) -> p half c t i", half=2, i=RUN)
            nc.scalar.copy(out=dst[:, 0], in_=source[:, 0])
            nc.vector.tensor_copy(out=dst[:, 1], in_=source[:, 1])
            nc.vector.quantize_mx(out=m_codes[:].bitcast(FP8X4), scales=m_plane[:], in_=m_bf[:])

        taken = {which: [] for which in RING_BANKS}

        def next_bank(which):
            turn = len(taken[which]) % RING_BANKS[which]
            taken[which].append(turn)
            return psum.tile([P, PACK, CHUNK], F32, name="%s%d" % (which, turn))

        def stationary(name, a, t):
            cols = slice(t * P, (t + 1) * P)
            if name == "a":
                return w1_codes[a][:, cols].bitcast(FP8X4), w1_plane[a][:, cols]
            if name == "b":
                return w2_codes[:, a, 2 * t * P : 2 * (t + 1) * P].bitcast(FP4X4), w2_plane[:, a, cols]
            return w3_codes[:, a, cols].bitcast(FP8X4), w3_plane[:, a, cols]

        def moving(name, a, g, i):
            cols = slice(g * GROUP + i * CHUNK, g * GROUP + (i + 1) * CHUNK)
            codes = words[name, g, a][:, i * CHUNK : (i + 1) * CHUNK].bitcast(FP8X4)
            if name == "b" and a == 1:
                return codes, b_plane_pass1[:, cols]
            return codes, planes[name][ROWS * a : P, cols]

        sums = {}

        def product(name, g, which):
            for i in range(PER):
                bank = next_bank(which)
                for t in range(PACK):
                    for a in range(PASSES):
                        lhs, lhs_scale = stationary(name, a, t)
                        rhs, rhs_scale = moving(name, a, g, i)
                        nc.tensor.matmul_mx(
                            out=bank[:, t, :], lhsT=lhs, lhsT_scale=lhs_scale, rhs=rhs, rhs_scale=rhs_scale,
                            start=(a == 0), stop=(a == PASSES - 1),
                        )
                sums[name, g, i] = bank[:].rearrange("p t n -> p n t")

        def chunk_of(tile, i):
            return tile[:, i * BANK : (i + 1) * BANK].rearrange("p (n t) -> p n t", t=PACK)

        root, damp, b_kept, diff, h_mx = {}, {}, {}, {}, {}

        def inverse_root(g):
            square = ring.tile([P, PER * BANK], F32, name="square")
            for i in range(PER):
                nc.scalar.activation(out=chunk_of(square, i), in_=sums["c", g, i], func=ACT.Square)
            root[g] = ring.tile([P, PER * BANK], F32, name="root")
            nc.scalar.activation(out=root[g][:], in_=square[:], func=ACT.Abs_reciprocal_sqrt, bias=1.0)

        def damping(g):
            damp[g] = held([P, PER * BANK], F32, "damp%d" % g)
            nc.scalar.activation(out=damp[g][:], in_=root[g][:], func=ACT.Square)

        def keep_b(g):
            b_kept[g] = held([P, PER * BANK], F32, "b_kept%d" % g)
            for i in range(PER):
                nc.scalar.copy(out=chunk_of(b_kept[g], i), in_=sums["b", g, i])

        def difference(g):
            diff[g] = held([P, PER * BANK], F32, "diff%d" % g)
            for i in range(PER):
                nc.vector.tensor_tensor(
                    out=chunk_of(diff[g], i), in0=sums["a", g, i], in1=chunk_of(b_kept[g], i), op=ALU.subtract
                )

        def flux(piece):
            g, i, count = piece
            cols = slice(i * BANK, (i + count) * BANK)
            h_bf = ring.tile([P, count * BANK], BF16, name="h_bf", align_bytes=64)
            nc.vector.tensor_tensor(out=h_bf[:], in0=diff[g][:, cols], in1=damp[g][:, cols], op=ALU.mult)
            codes = held([P, count * CHUNK], U32, "h_codes%d_%d" % (g, i))
            plane = held([P, count * CHUNK], U8, "h_plane%d_%d" % (g, i))
            nc.vector.quantize_mx(out=codes[:].bitcast(FP8X4), scales=plane[:], in_=h_bf[:])
            h_mx[piece] = (codes, plane)

        out_rows = out.rearrange("(u p) j -> p u j", p=P)
        updates = {}

        def update(piece, which):
            codes, plane = h_mx[piece]
            per_bank = PACK // piece[2]
            updates[piece] = []
            for first in range(0, N_TILES, per_bank):
                bank = next_bank(which)[:].rearrange("p t n -> p (t n)").rearrange("p (u w) -> p u w", u=per_bank)
                for u in range(per_bank):
                    cols = slice((first + u) * P, (first + u + 1) * P)
                    nc.tensor.matmul_mx(
                        out=bank[:, u, :], lhsT=m_codes[:, cols].bitcast(FP8X4), lhsT_scale=m_plane[:, cols],
                        rhs=codes[:].bitcast(FP8X4), rhs_scale=plane[:], start=True, stop=True,
                    )
                updates[piece].append((first, bank))

        def store(piece, on_vector):
            g, i, count = piece
            per_bank, width, start = PACK // count, count * CHUNK, g * GROUP + i * CHUNK
            for first, bank in updates[piece]:
                result = held([P, per_bank, width], F32, "result%d_%d_%d" % (g, i, first))
                if on_vector:
                    spread = src_col[:, first : first + per_bank].unsqueeze(2).to_broadcast([P, per_bank, width])
                    nc.vector.tensor_tensor(out=result[:], in0=bank, in1=spread, op=ALU.add)
                else:
                    for u in range(per_bank):
                        nc.scalar.activation(
                            out=result[:, u, :], in_=bank[:, u, :], func=ACT.Identity,
                            bias=src_col[:, first + u : first + u + 1],
                        )
                nc.sync.dma_start(out=out_rows[:, first : first + per_bank, start : start + width], in_=result[:])

        early, late = range(GROUPS // 2), range(GROUPS // 2, GROUPS)
        whole = [(g, 0, PER) for g in range(GROUPS - 1)]
        last = [(GROUPS - 1, i, 1) for i in range(PER)]

        product("c", 0, "scalar")
        gather_after_first_c()
        product("c", 1, "scalar")
        product("b", 0, "scalar")
        product("b", 1, "vector")
        product("c", late[0], "scalar")
        for g in early:
            inverse_root(g)
            damping(g)
        for a in range(PASSES):
            prepare_w1(a)
        keep_b(0)
        product("b", late[0], "scalar")
        product("b", late[1], "spare")
        keep_b(1)
        product("a", 0, "vector")
        prepare_m()
        for g in early:
            difference(g)
            product("a", g + 1, "vector")
            flux(whole[g])

        inverse_root(late[0])
        product("c", late[1], "scalar")
        keep_b(late[0])
        update(whole[0], "scalar")
        damping(late[0])
        inverse_root(late[1])
        update(whole[1], "scalar")
        keep_b(late[1])
        store(whole[0], on_vector=False)
        damping(late[1])

        difference(late[0])
        product("a", late[1], "vector")
        flux(whole[late[0]])
        update(whole[late[0]], "spare")
        store(whole[1], on_vector=False)
        difference(late[1])
        for piece in last:
            flux(piece)
        for piece in last:
            update(piece, "scalar")
        store(whole[late[0]], on_vector=False)
        for piece in last:
            store(piece, on_vector=True)
